import numpy as np
import ml_dtypes


def mxq(x, axis, fmt="e4m3"):
    dtype, down = {"e4m3": (ml_dtypes.float8_e4m3fn, 7), "e5m2": (ml_dtypes.float8_e5m2, 14)}[fmt]
    v = np.moveaxis(np.asarray(x, np.float32).astype(ml_dtypes.bfloat16).astype(np.float64), axis, -1)
    blocks = v.reshape(v.shape[:-1] + (-1, 32))
    amax = np.abs(blocks).max(-1, keepdims=True)
    byte = np.maximum(np.where(amax > 0, np.frexp(amax)[1] - 1 + 127, 0) - down, 1)
    scale = np.exp2(byte - 127.0)
    codes = (blocks / scale).astype(np.float32).astype(dtype).astype(np.float64)
    return np.moveaxis((codes * scale).reshape(v.shape), -1, axis)


WIDE = False


def mx_kscale(k):
    if not WIDE:
        return np.ones(k)
    levels = np.array([10, -10, 5, -5, 0])
    if k % 512:
        return np.exp2(np.random.permutation(np.resize(levels, k // 32))).repeat(32)
    a = np.empty((k // 512, 16))
    for p in range(k // 512):
        a[p, :8] = np.random.permutation(np.resize(levels, 8))
        for g in range(8):
            far = levels[np.abs(levels - a[p, g]) >= 10]
            a[p, g + 8] = far[np.random.randint(len(far))]
    return np.exp2(a.ravel()).repeat(32)


def f64(x):
    return np.asarray(x).astype(np.float64)


def striped(idx):
    return np.tile(idx.reshape(-1, 16).T, (8, 1)).astype(np.uint16)


def unstriped(offs):
    return offs[:16].T.reshape(-1).astype(np.int64)


E2M1 = np.array([0.0, 0.5, 1.0, 1.5, 2.0, 3.0, 4.0, 6.0, -0.0, -0.5, -1.0, -1.5, -2.0, -3.0, -4.0, -6.0])


def pack_weight(w, fmt):
    k, n = w.shape
    w = f64(np.asarray(w, np.float32).astype(ml_dtypes.bfloat16)).reshape(k // 32, 32, n)
    amax = np.abs(w).max(1)
    if fmt == "e4m3":
        byte = np.frexp(amax)[1] - 1 + 127 - 7
    else:
        mant, ex = np.frexp(amax / 6.0)
        byte = np.where(mant > 0.5, ex, ex - 1) + 127
    byte = np.clip(np.where(amax > 0, byte, 1), 1, 254)
    scaled = (w * np.exp2(127.0 - byte)[:, None, :]).reshape(k, n).astype(np.float32)
    by_word = np.ascontiguousarray(scaled.reshape(k // 512, 128, 4, n).transpose(0, 1, 3, 2))
    if fmt == "e4m3":
        words = by_word.astype(ml_dtypes.float8_e4m3fn).view(np.uint8)
    else:
        c = by_word.astype(ml_dtypes.float4_e2m1fn).view(np.uint8) & 0xF
        words = (c[..., 0::2] | (c[..., 1::2] << 4)).reshape(k // 512, 128, 2 * n)
    return np.ascontiguousarray(words), np.ascontiguousarray(byte.astype(np.uint8).reshape(k // 512, 16, n))


def unpack_weight(words, scales, fmt):
    g, _, n = scales.shape
    words = np.ascontiguousarray(words).reshape(g, 128, n, -1)
    if fmt == "e4m3":
        vals = words.view(ml_dtypes.float8_e4m3fn).astype(np.float64)
    else:
        nib = np.empty((g, 128, n, 4), np.uint8)
        nib[..., 0::2] = words & 0xF
        nib[..., 1::2] = words >> 4
        vals = E2M1[nib]
    vals = vals * np.repeat(np.exp2(scales.astype(np.float64) - 127.0), 8, axis=1)[..., None]
    return vals.transpose(0, 1, 3, 2).reshape(g * 512, n)


def gelu(v):
    return 0.5 * v * (1.0 + np.tanh(np.sqrt(2.0 / np.pi) * (v + 0.044715 * v**3)))


K, KA, KB, H, T, S, P = 1536, 1024, 512, 1024, 4096, 1024, 512


def setup_inputs():
    n = np.random.standard_normal
    s = mx_kscale(K)[:, None]
    u = mx_kscale(H)
    tab_words, tab_scales = pack_weight(n((K, T)) * s, "e4m3")
    w4_words, w4_scales = pack_weight(1.3 * n((KA, H)) / np.sqrt(K) / s[:KA], "e2m1")
    w1 = (1.3 * n((KB, H)) / np.sqrt(K) / s[KA:]).astype(np.float32)
    gain = (np.exp(0.3 * n(H)) * u).astype(np.float32)
    pay = (3.0 * n(H) / np.sqrt(H) / u ** 2).astype(np.float32)
    base = (0.8 * n(P)).astype(np.float32)
    return {
        "tab_words": tab_words, "tab_scales": tab_scales,
        "offs": striped(np.random.permutation(T)[:S]),
        "w4_words": w4_words, "w4_scales": w4_scales,
        "w1": w1, "gain": gain,
        "pos1": striped(np.random.permutation(S)[:P]),
        "pos2": striped(np.random.permutation(S)[:P]),
        "pay": pay, "base": base,
    }


def reference(tab_words, tab_scales, offs, w4_words, w4_scales, w1, gain, pos1, pos2, pay, base):
    v = unpack_weight(tab_words, tab_scales, "e4m3")[:, unstriped(offs)]
    w4 = unpack_weight(w4_words, w4_scales, "e2m1")
    w1q = mxq(f64(w1), 0, "e4m3")
    d = w4.T @ v[:KA] + w1q.T @ v[KA:]
    h = f64(gain)[:, None] * np.tanh(d)
    x1 = h[:, unstriped(pos1)]
    x2 = np.abs(h[:, unstriped(pos2)]) * f64(pay)[:, None]
    e = mxq(x1, 0, "e4m3").T @ mxq(x2, 0, "e4m3")
    a = e + f64(base)[:, None]
    return 1.0 / (1.0 + np.exp(-a))

@@ -1,0 +1,315 @@
+from contextlib import ExitStack
+
+import concourse.mybir as mybir
+from concourse.masks import make_identity
+
+K, KA, KB, H, T, S, NP = 1536, 1024, 512, 1024, 4096, 1024, 512
+FLOPS = 2 * K * H * S + 2 * H * NP * NP
+
+F32 = mybir.dt.float32
+BF16 = mybir.dt.bfloat16
+I32 = mybir.dt.int32
+U32 = mybir.dt.uint32
+U16 = mybir.dt.uint16
+U8 = mybir.dt.uint8
+FP8X4 = mybir.dt.float8_e4m3fn_x4
+FP4X4 = mybir.dt.float4_e2m1fn_x4
+ACT = mybir.ActivationFunctionType
+ALU = mybir.AluOpType
+
+P = 128
+NB = 512
+LAST_CHUNKS = ((0, 256), (256, 384), (384, 512))
+
+
+def tile_list_deck_synergy_chart_kernel(
+    tc, tab_words, tab_scales, offs, w4_words, w4_scales, w1, gain, pos1, pos2, pay, base, out
+):
+    nc = tc.nc
+    with ExitStack() as ctx:
+        lists = ctx.enter_context(tc.tile_pool(name="lists", bufs=1))
+        sb = ctx.enter_context(tc.tile_pool(name="sb", bufs=1))
+        ps = ctx.enter_context(tc.psum_pool(name="ps", bufs=1))
+
+        def tile(name, shape, dtype, tag=None):
+            return sb.tile(shape, dtype, name=name, tag=tag or name, align_bytes=64)
+
+        def bank(name, number, shape):
+            return ps.tile(shape, F32, name=name, tag="bank%d" % number)
+
+        scale_win = []
+        for a, tag in enumerate((None, None, "slot_c")):
+            win = tile("scale_win%d" % a, [P, T // 4], I32, tag)
+            nc.vector.memset(win[:], 0)
+            scale_win.append(win)
+        rows = tile("rows", [P, 2 * P], F32, "slot_b")
+        nc.gpsimd.memset(rows[:], 0.0)
+        w4s_raw = tile("w4s_raw", [P, 2, H // 4], I32)
+        nc.vector.memset(w4s_raw[:], 0)
+        ident = tile("ident", [P, P], F32)
+        make_identity(nc, ident[:])
+        v_scales = tile("v_scales", [P, 3, S // 4], I32)
+        nc.gpsimd.memset(v_scales[:], 0)
+
+        offs_sb = lists.tile([P, S // 16], U16, name="offs_sb")
+        pos2_sb = lists.tile([P, NP // 16], U16, name="pos2_sb")
+        pos1_sb = lists.tile([P, NP // 16], U16, name="pos1_sb")
+        nc.sync.dma_start(offs_sb[:], offs)
+
+        w4_i32 = w4_words.bitcast(I32)
+        w1_rows = w1.rearrange("(p j) c -> p j c", j=4)
+
+        def load_w4(b, tag):
+            raw = tile("w4_raw%d" % b, [P, 2, 256], I32, tag)
+            nc.sync.dma_start(raw[:], w4_i32[:, :, 256 * b : 256 * (b + 1)].rearrange("a p w -> p a w"))
+            return raw
+
+        def load_w1(b, tag):
+            raw = tile("w1_raw%d" % b, [P, 4, NB], F32, tag)
+            nc.sync.dma_start(raw[:], w1_rows[:, :, NB * b : NB * (b + 1)])
+            return raw
+
+        w4_raw = [load_w4(0, "slot_a")]
+        w1_raw = [load_w1(0, "slot_d")]
+        nc.sync.dma_start(pos2_sb[:], pos2)
+        nc.sync.dma_start(pos1_sb[:], pos1)
+        nc.scalar.dma_start(
+            rows[0:4, :].rearrange("t (x i) -> t x i", i=8), gain.rearrange("(x t i) -> t x i", t=4, i=8)
+        )
+        nc.scalar.dma_start(
+            rows[4:8, :].rearrange("t (x i) -> t x i", i=8), pay.rearrange("(x t i) -> t x i", t=4, i=8)
+        )
+        nc.scalar.dma_start(rows[8:12, 0:P], base.rearrange("(c p) -> c p", p=P))
+        for a in range(3):
+            nc.scalar.dma_start(scale_win[a][0:P:8, :], tab_scales[a].bitcast(I32))
+        w4s_i32 = w4_scales.bitcast(I32)
+        for q in range(4):
+            nc.scalar.dma_start(
+                w4s_raw[32 * q : 32 * q + 4, :, :], w4s_i32[:, 4 * q : 4 * q + 4, :].rearrange("a r w -> r a w")
+            )
+
+        def order_w4(b):
+            dst = tile("w4_%d" % b, [P, 2, 4, 64], I32)
+            nc.vector.tensor_copy(
+                dst[:].rearrange("p a t (q w) -> p a t q w", w=4),
+                w4_raw[b][:].rearrange("p a (q t w) -> p a t q w", t=4, w=4),
+            )
+            return dst
+
+        def round_w1(b, t, copy):
+            dst = tile("w1_bf%d_%d" % (b, t), [P, P * 4], BF16)
+            copy(
+                dst[:].rearrange("p (q h l j) -> p q h j l", h=2, l=4, j=4),
+                w1_raw[b][:].rearrange("p j (q t h l) -> p t q h j l", t=4, h=2, l=4)[:, t],
+            )
+            return dst
+
+        def quantize(name, src, width):
+            codes = tile(name + "_codes", [P, width], U32)
+            scales = tile(name + "_scales", [P, width], U8)
+            nc.vector.quantize_mx(out=codes[:].bitcast(FP8X4), scales=scales[:], in_=src)
+            return codes, scales
+
+        def w4_pass(acc, w4_b, b, t, a, n):
+            cols = slice(NB * n, NB * (n + 1))
+            nc.tensor.matmul_mx(
+                out=acc[:],
+                lhsT=w4_b[:, a, t, :].bitcast(FP4X4),
+                lhsT_scale=w4s[:, 2 * a + b, t, :].bitcast(U8),
+                rhs=v_words[a][:, cols].bitcast(FP8X4),
+                rhs_scale=v_scales[:, a, :].bitcast(U8)[:, cols],
+                start=(a == 0),
+                stop=False,
+            )
+
+        def w1_pass(acc, w1q, n):
+            cols = slice(NB * n, NB * (n + 1))
+            nc.tensor.matmul_mx(
+                out=acc[:],
+                lhsT=w1q[0][:].bitcast(FP8X4),
+                lhsT_scale=w1q[1][:],
+                rhs=v_words[2][:, cols].bitcast(FP8X4),
+                rhs_scale=v_scales[:, 2, :].bitcast(U8)[:, cols],
+                start=False,
+                stop=True,
+            )
+
+        def tanh_rows(s, accs):
+            th = tile("tanh%d" % s, [P, S], F32)
+            for n in range(2):
+                nc.scalar.activation(th[:, NB * n : NB * (n + 1)], accs[n][:], ACT.Tanh)
+            return th
+
+        def pick(dst, th, pos_sb, factor, m0, m1):
+            nc.vector.tensor_tensor(
+                dst, th[:].indirect(pos_sb[:, m0 // 16 : m1 // 16]), factor[:, 0 : m1 - m0], ALU.mult
+            )
+
+        def weave(dst, src, func):
+            nc.scalar.activation(
+                dst.rearrange("p (c i t) -> p c t i", i=4, t=4), src.rearrange("p t (c i) -> p c t i", i=4), func
+            )
+
+        def apply_sign(dst, src, b):
+            nc.vector.tensor_tensor(
+                dst.rearrange("p (x y) -> p x y", y=256),
+                src.rearrange("p (x y) -> p x y", y=256),
+                signs[:, b].rearrange("p c t -> p (c t)").unsqueeze(1).to_broadcast([P, NP * 4 // 256, 256]),
+                ALU.mult,
+            )
+
+        w4_0 = order_w4(0)
+        w1q0 = [quantize("w1q0_%d" % t, round_w1(0, t, nc.scalar.copy)[:], P) for t in range(4)]
+
+        rows_t = bank("rows_t", 7, [P, 2, P])
+        for b in range(2):
+            nc.tensor.transpose(rows_t[:, b, :], rows[:, P * b : P * (b + 1)], ident[:])
+        coef = tile("coef", [P, 2, 12], F32)
+        nc.scalar.copy(coef[:], rows_t[:, :, 0:12])
+        gain_pay = tile("gain_pay", [P, 2, 4], F32)
+        nc.vector.tensor_tensor(gain_pay[:], coef[:, :, 0:4], coef[:, :, 4:8], ALU.mult)
+        pay_pos = tile("pay_pos", [P, 2, 4], F32)
+        nc.vector.tensor_scalar(pay_pos[:], coef[:, :, 4:8], 0.0, None, ALU.is_ge)
+        pay_sign = tile("pay_sign", [P, 2, 4], F32)
+        nc.vector.tensor_scalar(pay_sign[:], pay_pos[:], 2.0, -1.0, ALU.mult, ALU.add)
+        half_base = tile("half_base", [P, 4], F32)
+        nc.vector.tensor_scalar(half_base[:], coef[:, 0, 8:12], 0.5, None, ALU.mult)
+
+        def load_table(a, tag):
+            words = tile("table%d" % a, [P, T], I32, tag)
+            nc.sync.dma_start(words[:], tab_words[a].rearrange("p t i -> p (t i)").bitcast(I32))
+            return words
+
+        table = [load_table(0, "slot_a"), load_table(1, "slot_b")]
+
+        f1 = []
+        f2 = []
+        for s in range(8):
+            b, t = divmod(s, 4)
+            f2_s = tile("f2_%d" % s, [P, NP], F32)
+            nc.scalar.copy(f2_s[:], gain_pay[:, b, t : t + 1].to_broadcast([P, NP]))
+            f1_s = tile("f1_%d" % s, [P, NP], F32)
+            nc.scalar.copy(f1_s[:], coef[:, b, t : t + 1].to_broadcast([P, NP]))
+            f1.append(f1_s)
+            f2.append(f2_s)
+        signs = tile("signs", [P, 2, 64, 4], BF16)
+        nc.scalar.copy(signs[:], pay_sign[:].unsqueeze(2).to_broadcast([P, 2, 64, 4]))
+
+        picked_scales = tile("picked_scales", [P, 3, S], U8)
+        for a in range(3):
+            nc.vector.tensor_copy(picked_scales[:, a, :], scale_win[a][:].bitcast(U8).indirect(offs_sb[:]))
+        for q in range(4):
+            nc.sync.dma_start(
+                v_scales[32 * q : 32 * q + 4, :, :], picked_scales[32 * q : 32 * q + 32 : 8, :, :].bitcast(I32)
+            )
+        table.append(load_table(2, "slot_c"))
+        v_words = []
+        for a in range(3):
+            v_a = tile("v_words%d" % a, [P, S], U32)
+            step = NB if a == 2 else S
+            for j in range(0, S, step):
+                nc.vector.tensor_copy(
+                    v_a[:, j : j + step], table[a][:].bitcast(U32).indirect(offs_sb[:, j // 16 : (j + step) // 16])
+                )
+            v_words.append(v_a)
+        w4_raw.append(load_w4(1, "slot_a"))
+        w1_raw.append(load_w1(1, "slot_b"))
+
+        w4s = tile("w4s", [P, 4, 4, 32], I32)
+        nc.vector.tensor_copy(
+            w4s[:].rearrange("p x t (q w) -> p x t q w", w=2),
+            w4s_raw[:].rearrange("p a (b q t w) -> p (a b) t q w", b=2, t=4, w=2),
+        )
+
+        accs = [[bank("acc%d_%d" % (t, n), 2 * t + n, [P, NB]) for n in range(2)] for t in range(4)]
+        for a in range(2):
+            for t in range(4):
+                for n in range(2):
+                    w4_pass(accs[t][n], w4_0, 0, t, a, n)
+        for n in range(2):
+            for t in range(4):
+                w1_pass(accs[t][n], w1q0[t], n)
+        w4_1 = order_w4(1)
+
+        g2 = [tile("g2_0", [P, 4, NP], F32, "slot_a")]
+        g1_0 = tile("g1_0", [P, 4, NP], F32, "slot_c")
+        th = []
+        accs1 = []
+        for t in range(4):
+            th.append(tanh_rows(t, accs[t]))
+            w1q = quantize("w1q1_%d" % t, round_w1(1, t, nc.scalar.copy)[:], P)
+            pair = [bank("acc%d_%d" % (4 + t, n), 2 * t + n, [P, NB]) for n in range(2)]
+            for n in range(2):
+                for a in range(2):
+                    w4_pass(pair[n], w4_1, 1, t, a, n)
+                w1_pass(pair[n], w1q, n)
+            accs1.append(pair)
+            pick(g2[0][:, t, :], th[t], pos2_sb, f2[t], 0, NP)
+            pick(g1_0[:, t, :], th[t], pos1_sb, f1[t], 0, NP)
+
+        g2.append(tile("g2_1", [P, 4, NP], F32, "slot_d"))
+        th.append(tanh_rows(4, accs1[0]))
+        pick(g2[1][:, 0, :], th[4], pos2_sb, f2[4], 0, NP)
+        th.append(tanh_rows(5, accs1[1]))
+        pick(g2[1][:, 1, :], th[5], pos2_sb, f2[5], 0, NP)
+        x2_0 = tile("x2_0", [P, NP * 4], BF16)
+        weave(x2_0[:], g2[0][:], ACT.Abs)
+        th.append(tanh_rows(6, accs1[2]))
+        pick(g2[1][:, 2, :], th[6], pos2_sb, f2[6], 0, NP)
+        th.append(tanh_rows(7, accs1[3]))
+        pick(g2[1][:, 3, :], th[7], pos2_sb, f2[7], 0, NP)
+        apply_sign(x2_0[:], x2_0[:], 0)
+        x2q = [quantize("x2q0", x2_0[:], NP)]
+        x1_0 = tile("x1_0", [P, NP * 4], BF16)
+        weave(x1_0[:], g1_0[:], ACT.Copy)
+        x1q0 = quantize("x1q0", x1_0[:], NP)
+
+        e = [bank("e%d" % c, c, [P, NP]) for c in range(4)]
+        for c in range(4):
+            nc.tensor.matmul_mx(
+                out=e[c][:],
+                lhsT=x1q0[0][:, P * c : P * (c + 1)].bitcast(FP8X4),
+                lhsT_scale=x1q0[1][:, P * c : P * (c + 1)],
+                rhs=x2q[0][0][:].bitcast(FP8X4),
+                rhs_scale=x2q[0][1][:],
+                start=True,
+                stop=False,
+            )
+
+        x2_abs = tile("x2_abs", [P, NP * 4], BF16)
+        x2_1 = tile("x2_1", [P, NP * 4], BF16)
+        weave(x2_abs[:], g2[1][:], ACT.Abs)
+
+        first = tile("g1_first", [P, 4 * 256], F32, "f2_7")
+        for t in range(4):
+            pick(first[:, 256 * t : 256 * (t + 1)], th[4 + t], pos1_sb, f1[4 + t], 0, 256)
+        apply_sign(x2_1[:], x2_abs[:], 1)
+        x2q.append(quantize("x2q1", x2_1[:], NP))
+        rest = tile("g1_rest", [P, 4 * 256], F32, "x2_abs")
+
+        for index, (m0, m1) in enumerate(LAST_CHUNKS):
+            width = m1 - m0
+            if index == 0:
+                g = first[:]
+            else:
+                g = rest[:, 4 * (m0 - 256) : 4 * (m1 - 256)]
+                for t in range(4):
+                    pick(g[:, width * t : width * (t + 1)], th[4 + t], pos1_sb, f1[4 + t], m0, m1)
+            x1_c = tile("x1_1_%d" % index, [P, width * 4], BF16)
+            weave(x1_c[:], g.rearrange("p (t m) -> p t m", t=4), ACT.Copy)
+            codes, scales = quantize("x1q1_%d" % index, x1_c[:], width)
+            for c in range(m0 // P, m1 // P):
+                cols = slice(P * c - m0, P * (c + 1) - m0)
+                nc.tensor.matmul_mx(
+                    out=e[c][:],
+                    lhsT=codes[:, cols].bitcast(FP8X4),
+                    lhsT_scale=scales[:, cols],
+                    rhs=x2q[1][0][:].bitcast(FP8X4),
+                    rhs_scale=x2q[1][1][:],
+                    start=False,
+                    stop=True,
+                )
+                res = tile("res%d" % c, [P, NP], F32)
+                nc.scalar.activation(res[:], e[c][:], ACT.Tanh, bias=half_base[:, c : c + 1], scale=0.5)
+                nc.vector.tensor_scalar(res[:], res[:], 0.5, 0.5, ALU.mult, ALU.add)
+                nc.sync.dma_start(out[P * c : P * (c + 1), :], res[:])

@@ -19,7 +19,7 @@ ALU = mybir.AluOpType
 
 P = 128
 NB = 512
-LAST_CHUNKS = ((0, 256), (256, 384), (384, 512))
+PLACES = {"slot_a": 0, "slot_aw": 15 * 1024, "slot_w": 16 * 1024, "slot_b": 18 * 1024, "slot_c": 34 * 1024}
 
 
 def tile_list_deck_synergy_chart_kernel(
@@ -29,23 +29,21 @@ def tile_list_deck_synergy_chart_kernel(
     with ExitStack() as ctx:
         lists = ctx.enter_context(tc.tile_pool(name="lists", bufs=1))
         sb = ctx.enter_context(tc.tile_pool(name="sb", bufs=1))
+        shared = ctx.enter_context(tc.tile_pool(name="shared", bufs=1))
         ps = ctx.enter_context(tc.psum_pool(name="ps", bufs=1))
 
         def tile(name, shape, dtype, tag=None):
+            if tag in PLACES:
+                return shared.tile(shape, dtype, name=name, align_bytes=64, offset=PLACES[tag])
             return sb.tile(shape, dtype, name=name, tag=tag or name, align_bytes=64)
 
         def bank(name, number, shape):
             return ps.tile(shape, F32, name=name, tag="bank%d" % number)
 
-        scale_win = []
-        for a, tag in enumerate((None, None, "slot_c")):
-            win = tile("scale_win%d" % a, [P, T // 4], I32, tag)
-            nc.vector.memset(win[:], 0)
-            scale_win.append(win)
+        scale_win = tile("scale_win", [P, 3, T // 4], I32, "slot_d")
+        nc.vector.memset(scale_win[:], 0)
         rows = tile("rows", [P, 2 * P], F32, "slot_b")
         nc.gpsimd.memset(rows[:], 0.0)
-        w4s_raw = tile("w4s_raw", [P, 2, H // 4], I32)
-        nc.vector.memset(w4s_raw[:], 0)
         ident = tile("ident", [P, P], F32)
         make_identity(nc, ident[:])
         v_scales = tile("v_scales", [P, 3, S // 4], I32)
@@ -69,10 +67,16 @@ def tile_list_deck_synergy_chart_kernel(
             nc.sync.dma_start(raw[:], w1_rows[:, :, NB * b : NB * (b + 1)])
             return raw
 
-        w4_raw = [load_w4(0, "slot_a")]
-        w1_raw = [load_w1(0, "slot_d")]
+        def load_table(a, tag):
+            words = tile("table%d" % a, [P, T], I32, tag)
+            nc.sync.dma_start(words[:], tab_words[a].rearrange("p t i -> p (t i)").bitcast(I32))
+            return words
+
         nc.sync.dma_start(pos2_sb[:], pos2)
         nc.sync.dma_start(pos1_sb[:], pos1)
+        w4_raw = [load_w4(0, "slot_aw")]
+        w1_raw = [load_w1(0, "slot_c")]
+        nc.sync.dma_start(scale_win[0:P:8, :, :], tab_scales.bitcast(I32).rearrange("a q w -> q a w"))
         nc.scalar.dma_start(
             rows[0:4, :].rearrange("t (x i) -> t x i", i=8), gain.rearrange("(x t i) -> t x i", t=4, i=8)
         )
@@ -80,14 +84,6 @@ def tile_list_deck_synergy_chart_kernel(
             rows[4:8, :].rearrange("t (x i) -> t x i", i=8), pay.rearrange("(x t i) -> t x i", t=4, i=8)
         )
         nc.scalar.dma_start(rows[8:12, 0:P], base.rearrange("(c p) -> c p", p=P))
-        for a in range(3):
-            nc.scalar.dma_start(scale_win[a][0:P:8, :], tab_scales[a].bitcast(I32))
-        w4s_i32 = w4_scales.bitcast(I32)
-        for q in range(4):
-            nc.scalar.dma_start(
-                w4s_raw[32 * q : 32 * q + 4, :, :], w4s_i32[:, 4 * q : 4 * q + 4, :].rearrange("a r w -> r a w")
-            )
-
         def order_w4(b):
             dst = tile("w4_%d" % b, [P, 2, 4, 64], I32)
             nc.vector.tensor_copy(
@@ -96,9 +92,9 @@ def tile_list_deck_synergy_chart_kernel(
             )
             return dst
 
-        def round_w1(b, t, copy):
-            dst = tile("w1_bf%d_%d" % (b, t), [P, P * 4], BF16)
-            copy(
+        def round_w1(b, t, tag):
+            dst = tile("w1_bf%d_%d" % (b, t), [P, P * 4], BF16, tag)
+            nc.scalar.copy(
                 dst[:].rearrange("p (q h l j) -> p q h j l", h=2, l=4, j=4),
                 w1_raw[b][:].rearrange("p j (q t h l) -> p t q h j l", t=4, h=2, l=4)[:, t],
             )
@@ -159,7 +155,14 @@ def tile_list_deck_synergy_chart_kernel(
             )
 
         w4_0 = order_w4(0)
-        w1q0 = [quantize("w1q0_%d" % t, round_w1(0, t, nc.scalar.copy)[:], P) for t in range(4)]
+        table = [load_table(0, "slot_a")]
+        w4s_raw = tile("w4s_raw", [P, 2, H // 4], I32, "slot_w")
+        nc.gpsimd.memset(w4s_raw[:], 0)
+        w4s_i32 = w4_scales.bitcast(I32)
+        for q in range(4):
+            nc.scalar.dma_start(
+                w4s_raw[32 * q : 32 * q + 4, :, :], w4s_i32[:, 4 * q : 4 * q + 4, :].rearrange("a r w -> r a w")
+            )
 
         rows_t = bank("rows_t", 7, [P, 2, P])
         for b in range(2):
@@ -167,42 +170,42 @@ def tile_list_deck_synergy_chart_kernel(
         coef = tile("coef", [P, 2, 12], F32)
         nc.scalar.copy(coef[:], rows_t[:, :, 0:12])
         gain_pay = tile("gain_pay", [P, 2, 4], F32)
-        nc.vector.tensor_tensor(gain_pay[:], coef[:, :, 0:4], coef[:, :, 4:8], ALU.mult)
+        nc.gpsimd.tensor_tensor(gain_pay[:], coef[:, :, 0:4], coef[:, :, 4:8], ALU.mult)
         pay_pos = tile("pay_pos", [P, 2, 4], F32)
-        nc.vector.tensor_scalar(pay_pos[:], coef[:, :, 4:8], 0.0, None, ALU.is_ge)
+        nc.gpsimd.tensor_scalar(pay_pos[:], coef[:, :, 4:8], 0.0, None, ALU.is_ge)
         pay_sign = tile("pay_sign", [P, 2, 4], F32)
-        nc.vector.tensor_scalar(pay_sign[:], pay_pos[:], 2.0, -1.0, ALU.mult, ALU.add)
-        half_base = tile("half_base", [P, 4], F32)
-        nc.vector.tensor_scalar(half_base[:], coef[:, 0, 8:12], 0.5, None, ALU.mult)
+        nc.gpsimd.tensor_scalar(pay_sign[:], pay_pos[:], 2.0, -1.0, ALU.mult, ALU.add)
 
-        def load_table(a, tag):
-            words = tile("table%d" % a, [P, T], I32, tag)
-            nc.sync.dma_start(words[:], tab_words[a].rearrange("p t i -> p (t i)").bitcast(I32))
-            return words
+        w1q0 = [quantize("w1q0_%d" % t, round_w1(0, t, None)[:], P) for t in range(4)]
 
-        table = [load_table(0, "slot_a"), load_table(1, "slot_b")]
+        table.append(load_table(1, "slot_b"))
+        table.append(load_table(2, "slot_c"))
 
         f1 = []
         f2 = []
-        for s in range(8):
-            b, t = divmod(s, 4)
-            f2_s = tile("f2_%d" % s, [P, NP], F32)
-            nc.scalar.copy(f2_s[:], gain_pay[:, b, t : t + 1].to_broadcast([P, NP]))
-            f1_s = tile("f1_%d" % s, [P, NP], F32)
-            nc.scalar.copy(f1_s[:], coef[:, b, t : t + 1].to_broadcast([P, NP]))
-            f1.append(f1_s)
-            f2.append(f2_s)
-        signs = tile("signs", [P, 2, 64, 4], BF16)
-        nc.scalar.copy(signs[:], pay_sign[:].unsqueeze(2).to_broadcast([P, 2, 64, 4]))
+
+        def spread_factors(b):
+            for t in range(4):
+                f1_s = tile("f1_%d" % (4 * b + t), [P, NP], F32)
+                nc.scalar.copy(f1_s[:], coef[:, b, t : t + 1].to_broadcast([P, NP]))
+                f1.append(f1_s)
+            for t in range(4):
+                f2_s = tile("f2_%d" % (4 * b + t), [P, NP], F32)
+                nc.scalar.copy(f2_s[:], gain_pay[:, b, t : t + 1].to_broadcast([P, NP]))
+                f2.append(f2_s)
+
+        spread_factors(0)
 
         picked_scales = tile("picked_scales", [P, 3, S], U8)
         for a in range(3):
-            nc.vector.tensor_copy(picked_scales[:, a, :], scale_win[a][:].bitcast(U8).indirect(offs_sb[:]))
+            nc.vector.tensor_copy(picked_scales[:, a, :], scale_win[:, a, :].bitcast(U8).indirect(offs_sb[:]))
         for q in range(4):
-            nc.sync.dma_start(
+            nc.scalar.dma_start(
                 v_scales[32 * q : 32 * q + 4, :, :], picked_scales[32 * q : 32 * q + 32 : 8, :, :].bitcast(I32)
             )
-        table.append(load_table(2, "slot_c"))
+        spread_factors(1)
+        signs = tile("signs", [P, 2, 64, 4], BF16)
+        nc.scalar.copy(signs[:], pay_sign[:].unsqueeze(2).to_broadcast([P, 2, 64, 4]))
         v_words = []
         for a in range(3):
             v_a = tile("v_words%d" % a, [P, S], U32)
@@ -237,7 +240,7 @@ def tile_list_deck_synergy_chart_kernel(
         accs1 = []
         for t in range(4):
             th.append(tanh_rows(t, accs[t]))
-            w1q = quantize("w1q1_%d" % t, round_w1(1, t, nc.scalar.copy)[:], P)
+            w1q = quantize("w1q1_%d" % t, round_w1(1, t, "w1q0_%d_codes" % t)[:], P)
             pair = [bank("acc%d_%d" % (4 + t, n), 2 * t + n, [P, NB]) for n in range(2)]
             for n in range(2):
                 for a in range(2):
@@ -264,52 +267,55 @@ def tile_list_deck_synergy_chart_kernel(
         weave(x1_0[:], g1_0[:], ACT.Copy)
         x1q0 = quantize("x1q0", x1_0[:], NP)
 
-        e = [bank("e%d" % c, c, [P, NP]) for c in range(4)]
-        for c in range(4):
+        def product_pass(acc, x1q, cols, x2q_b, j0, j1, first_pass):
             nc.tensor.matmul_mx(
-                out=e[c][:],
-                lhsT=x1q0[0][:, P * c : P * (c + 1)].bitcast(FP8X4),
-                lhsT_scale=x1q0[1][:, P * c : P * (c + 1)],
-                rhs=x2q[0][0][:].bitcast(FP8X4),
-                rhs_scale=x2q[0][1][:],
-                start=True,
-                stop=False,
+                out=acc[:],
+                lhsT=x1q[0][:, cols].bitcast(FP8X4),
+                lhsT_scale=x1q[1][:, cols],
+                rhs=x2q_b[0][:, j0:j1].bitcast(FP8X4),
+                rhs_scale=x2q_b[1][:, j0:j1],
+                start=first_pass,
+                stop=not first_pass,
             )
+
+        e = [[(bank("e%d" % c, c, [P, NP]), 0, NP)] for c in range(3)]
+        e.append([(bank("e3_%d" % h, 3 + h, [P, NP // 2]), NP // 2 * h, NP // 2 * (h + 1)) for h in range(2)])
+        for c in range(4):
+            for acc, j0, j1 in e[c]:
+                product_pass(acc, x1q0, slice(P * c, P * (c + 1)), x2q[0], j0, j1, True)
 
         x2_abs = tile("x2_abs", [P, NP * 4], BF16)
         x2_1 = tile("x2_1", [P, NP * 4], BF16)
         weave(x2_abs[:], g2[1][:], ACT.Abs)
 
-        first = tile("g1_first", [P, 4 * 256], F32, "f2_7")
+        def finish_product(c, x1q, cols):
+            for acc, j0, j1 in e[c]:
+                product_pass(acc, x1q, cols, x2q[1], j0, j1, False)
+
+        def finish_rows(c):
+            for acc, j0, j1 in e[c]:
+                res = tile("res%d_%d" % (c, j0), [P, j1 - j0], F32)
+                nc.scalar.activation(res[:], acc[:], ACT.Sigmoid, bias=coef[:, 0, 8 + c : 9 + c])
+                nc.sync.dma_start(out[P * c : P * (c + 1), j0:j1], res[:])
+
+        first = tile("g1_first", [P, 4, 2 * P], F32, "f2_7")
         for t in range(4):
-            pick(first[:, 256 * t : 256 * (t + 1)], th[4 + t], pos1_sb, f1[4 + t], 0, 256)
+            pick(first[:, t, :], th[4 + t], pos1_sb, f1[4 + t], 0, 2 * P)
         apply_sign(x2_1[:], x2_abs[:], 1)
         x2q.append(quantize("x2q1", x2_1[:], NP))
-        rest = tile("g1_rest", [P, 4 * 256], F32, "x2_abs")
+        x1_first = tile("x1_first", [P, 2 * P * 4], BF16)
+        weave(x1_first[:], first[:], ACT.Copy)
+        x1q_first = quantize("x1q_first", x1_first[:], 2 * P)
+        for c in range(2):
+            finish_product(c, x1q_first, slice(P * c, P * (c + 1)))
 
-        for index, (m0, m1) in enumerate(LAST_CHUNKS):
-            width = m1 - m0
-            if index == 0:
-                g = first[:]
-            else:
-                g = rest[:, 4 * (m0 - 256) : 4 * (m1 - 256)]
-                for t in range(4):
-                    pick(g[:, width * t : width * (t + 1)], th[4 + t], pos1_sb, f1[4 + t], m0, m1)
-            x1_c = tile("x1_1_%d" % index, [P, width * 4], BF16)
-            weave(x1_c[:], g.rearrange("p (t m) -> p t m", t=4), ACT.Copy)
-            codes, scales = quantize("x1q1_%d" % index, x1_c[:], width)
-            for c in range(m0 // P, m1 // P):
-                cols = slice(P * c - m0, P * (c + 1) - m0)
-                nc.tensor.matmul_mx(
-                    out=e[c][:],
-                    lhsT=codes[:, cols].bitcast(FP8X4),
-                    lhsT_scale=scales[:, cols],
-                    rhs=x2q[1][0][:].bitcast(FP8X4),
-                    rhs_scale=x2q[1][1][:],
-                    start=False,
-                    stop=True,
-                )
-                res = tile("res%d" % c, [P, NP], F32)
-                nc.scalar.activation(res[:], e[c][:], ACT.Tanh, bias=half_base[:, c : c + 1], scale=0.5)
-                nc.vector.tensor_scalar(res[:], res[:], 0.5, 0.5, ALU.mult, ALU.add)
-                nc.sync.dma_start(out[P * c : P * (c + 1), :], res[:])
+        rest = tile("g1_rest", [P, 2, 4, P], F32, "x2_abs")
+        for c, tag in ((2, "x1q_first_codes"), (3, "x1q_first_scales")):
+            finish_rows(c - 2)
+            for t in range(4):
+                pick(rest[:, c - 2, t, :], th[4 + t], pos1_sb, f1[4 + t], P * c, P * (c + 1))
+            x1_c = tile("x1_rest%d" % c, [P, P * 4], BF16, tag)
+            weave(x1_c[:], rest[:, c - 2], ACT.Copy)
+            finish_product(c, quantize("x1q_rest%d" % c, x1_c[:], P), slice(0, P))
+        for c in range(2, 4):
+            finish_rows(c)

@@ -19,7 +19,16 @@ ALU = mybir.AluOpType
 
 P = 128
 NB = 512
-PLACES = {"slot_a": 0, "slot_aw": 15 * 1024, "slot_w": 16 * 1024, "slot_b": 18 * 1024, "slot_c": 34 * 1024}
+PLACES = {
+    "slot_a": 0,
+    "slot_a2": 4 * 1024,
+    "slot_aw": 15 * 1024,
+    "slot_w": 16 * 1024,
+    "slot_b": 18 * 1024,
+    "slot_bv": 29 * 1024,
+    "slot_v": 34 * 1024,
+    "slot_c": 37 * 1024,
+}
 
 
 def tile_list_deck_synergy_chart_kernel(
@@ -40,14 +49,14 @@ def tile_list_deck_synergy_chart_kernel(
         def bank(name, number, shape):
             return ps.tile(shape, F32, name=name, tag="bank%d" % number)
 
-        scale_win = tile("scale_win", [P, 3, T // 4], I32, "slot_d")
+        scale_win = tile("scale_win", [P, 3, T // 4], I32, "slot_c")
         nc.vector.memset(scale_win[:], 0)
-        rows = tile("rows", [P, 2 * P], F32, "slot_b")
+        vectors = tile("vectors", [32, H], F32)
+        nc.gpsimd.memset(vectors[:], 0.0)
+        rows = tile("rows", [P, 8, P], F32)
         nc.gpsimd.memset(rows[:], 0.0)
         ident = tile("ident", [P, P], F32)
         make_identity(nc, ident[:])
-        v_scales = tile("v_scales", [P, 3, S // 4], I32)
-        nc.gpsimd.memset(v_scales[:], 0)
 
         offs_sb = lists.tile([P, S // 16], U16, name="offs_sb")
         pos2_sb = lists.tile([P, NP // 16], U16, name="pos2_sb")
@@ -75,15 +84,11 @@ def tile_list_deck_synergy_chart_kernel(
         nc.sync.dma_start(pos2_sb[:], pos2)
         nc.sync.dma_start(pos1_sb[:], pos1)
         w4_raw = [load_w4(0, "slot_aw")]
-        w1_raw = [load_w1(0, "slot_c")]
+        w1_raw = [load_w1(0, "slot_bv")]
         nc.sync.dma_start(scale_win[0:P:8, :, :], tab_scales.bitcast(I32).rearrange("a q w -> q a w"))
-        nc.scalar.dma_start(
-            rows[0:4, :].rearrange("t (x i) -> t x i", i=8), gain.rearrange("(x t i) -> t x i", t=4, i=8)
-        )
-        nc.scalar.dma_start(
-            rows[4:8, :].rearrange("t (x i) -> t x i", i=8), pay.rearrange("(x t i) -> t x i", t=4, i=8)
-        )
-        nc.scalar.dma_start(rows[8:12, 0:P], base.rearrange("(c p) -> c p", p=P))
+        nc.scalar.dma_start(vectors[0:1, :], gain.rearrange("(o r) -> o r", o=1))
+        nc.scalar.dma_start(vectors[1:2, :], pay.rearrange("(o r) -> o r", o=1))
+        nc.scalar.dma_start(rows[32:36, 0, :], base.rearrange("(c p) -> c p", p=P))
         def order_w4(b):
             dst = tile("w4_%d" % b, [P, 2, 4, 64], I32)
             nc.vector.tensor_copy(
@@ -106,7 +111,7 @@ def tile_list_deck_synergy_chart_kernel(
             nc.vector.quantize_mx(out=codes[:].bitcast(FP8X4), scales=scales[:], in_=src)
             return codes, scales
 
-        def w4_pass(acc, w4_b, b, t, a, n):
+        def w4_pass(acc, w4_b, b, t, a, n, start, stop):
             cols = slice(NB * n, NB * (n + 1))
             nc.tensor.matmul_mx(
                 out=acc[:],
@@ -114,11 +119,11 @@ def tile_list_deck_synergy_chart_kernel(
                 lhsT_scale=w4s[:, 2 * a + b, t, :].bitcast(U8),
                 rhs=v_words[a][:, cols].bitcast(FP8X4),
                 rhs_scale=v_scales[:, a, :].bitcast(U8)[:, cols],
-                start=(a == 0),
-                stop=False,
+                start=start,
+                stop=stop,
             )
 
-        def w1_pass(acc, w1q, n):
+        def w1_pass(acc, w1q, n, start, stop):
             cols = slice(NB * n, NB * (n + 1))
             nc.tensor.matmul_mx(
                 out=acc[:],
@@ -126,8 +131,8 @@ def tile_list_deck_synergy_chart_kernel(
                 lhsT_scale=w1q[1][:],
                 rhs=v_words[2][:, cols].bitcast(FP8X4),
                 rhs_scale=v_scales[:, 2, :].bitcast(U8)[:, cols],
-                start=False,
-                stop=True,
+                start=start,
+                stop=stop,
             )
 
         def tanh_rows(s, accs):
@@ -159,53 +164,54 @@ def tile_list_deck_synergy_chart_kernel(
         w4s_raw = tile("w4s_raw", [P, 2, H // 4], I32, "slot_w")
         nc.gpsimd.memset(w4s_raw[:], 0)
         w4s_i32 = w4_scales.bitcast(I32)
-        for q in range(4):
-            nc.scalar.dma_start(
-                w4s_raw[32 * q : 32 * q + 4, :, :], w4s_i32[:, 4 * q : 4 * q + 4, :].rearrange("a r w -> r a w")
-            )
+        for r in range(4):
+            nc.scalar.dma_start(w4s_raw[r:P:32, :, :], w4s_i32[:, r:16:4, :].rearrange("a q w -> q a w"))
 
-        rows_t = bank("rows_t", 7, [P, 2, P])
+        w1_bf0 = [round_w1(0, t, None) for t in range(4)]
+
+        nc.scalar.copy(
+            rows[0:32].rearrange("v (b t) (q i) -> v b t q i", t=4, i=8),
+            vectors[:].rearrange("v (b q t i) -> v b t q i", b=2, t=4, i=8),
+        )
+        coef = tile("coef", [P, 2, 4, 2], F32)
+        base_col = tile("base_col", [P, 4], F32)
         for b in range(2):
-            nc.tensor.transpose(rows_t[:, b, :], rows[:, P * b : P * (b + 1)], ident[:])
-        coef = tile("coef", [P, 2, 12], F32)
-        nc.scalar.copy(coef[:], rows_t[:, :, 0:12])
-        gain_pay = tile("gain_pay", [P, 2, 4], F32)
-        nc.gpsimd.tensor_tensor(gain_pay[:], coef[:, :, 0:4], coef[:, :, 4:8], ALU.mult)
-        pay_pos = tile("pay_pos", [P, 2, 4], F32)
-        nc.gpsimd.tensor_scalar(pay_pos[:], coef[:, :, 4:8], 0.0, None, ALU.is_ge)
-        pay_sign = tile("pay_sign", [P, 2, 4], F32)
-        nc.gpsimd.tensor_scalar(pay_sign[:], pay_pos[:], 2.0, -1.0, ALU.mult, ALU.add)
-
-        w1q0 = [quantize("w1q0_%d" % t, round_w1(0, t, None)[:], P) for t in range(4)]
-
+            rows_t = bank("rows_t%d" % b, 6 + b, [P, 4, P])
+            for t in range(4):
+                nc.tensor.transpose(rows_t[:, t, :], rows[:, 4 * b + t, :], ident[:])
+            nc.scalar.copy(coef[:, b], rows_t[:, :, 0:2])
+            if b == 0:
+                nc.scalar.copy(base_col[:], rows_t[:, 0, 32:36])
         table.append(load_table(1, "slot_b"))
-        table.append(load_table(2, "slot_c"))
+        v_scales = tile("v_scales", [P, 3, S // 4], I32, "slot_v")
+        nc.gpsimd.memset(v_scales[:], 0)
 
         f1 = []
         f2 = []
 
-        def spread_factors(b):
-            for t in range(4):
-                f1_s = tile("f1_%d" % (4 * b + t), [P, NP], F32)
-                nc.scalar.copy(f1_s[:], coef[:, b, t : t + 1].to_broadcast([P, NP]))
-                f1.append(f1_s)
-            for t in range(4):
-                f2_s = tile("f2_%d" % (4 * b + t), [P, NP], F32)
-                nc.scalar.copy(f2_s[:], gain_pay[:, b, t : t + 1].to_broadcast([P, NP]))
-                f2.append(f2_s)
-
-        spread_factors(0)
+        for s in range(8):
+            b, t = divmod(s, 4)
+            f1_s = tile("f1_%d" % s, [P, NP], F32)
+            nc.scalar.copy(f1_s[:], coef[:, b, t, 0:1].to_broadcast([P, NP]))
+            f2_s = tile("f2_%d" % s, [P, NP], F32)
+            nc.scalar.activation(f2_s[:], f1_s[:], ACT.Copy, scale=coef[:, b, t, 1:2])
+            f1.append(f1_s)
+            f2.append(f2_s)
+        signs = tile("signs", [P, 2, 64, 4], BF16)
+        nc.scalar.activation(signs[:], coef[:, :, :, 1].unsqueeze(2).to_broadcast([P, 2, 64, 4]), ACT.Sign)
 
         picked_scales = tile("picked_scales", [P, 3, S], U8)
         for a in range(3):
             nc.vector.tensor_copy(picked_scales[:, a, :], scale_win[:, a, :].bitcast(U8).indirect(offs_sb[:]))
-        for q in range(4):
-            nc.scalar.dma_start(
-                v_scales[32 * q : 32 * q + 4, :, :], picked_scales[32 * q : 32 * q + 32 : 8, :, :].bitcast(I32)
-            )
-        spread_factors(1)
-        signs = tile("signs", [P, 2, 64, 4], BF16)
-        nc.scalar.copy(signs[:], pay_sign[:].unsqueeze(2).to_broadcast([P, 2, 64, 4]))
+        for r in range(4):
+            nc.sync.dma_start(v_scales[r:P:32, :, :], picked_scales[8 * r : P : 32, :, :].bitcast(I32))
+        table.append(load_table(2, "slot_c"))
+        w4s = tile("w4s", [P, 4, 4, 32], I32)
+        nc.vector.tensor_copy(
+            w4s[:].rearrange("p x t (q w) -> p x t q w", w=2),
+            w4s_raw[:].rearrange("p a (b q t w) -> p (a b) t q w", b=2, t=4, w=2),
+        )
+
         v_words = []
         for a in range(3):
             v_a = tile("v_words%d" % a, [P, S], U32)
@@ -218,23 +224,20 @@ def tile_list_deck_synergy_chart_kernel(
         w4_raw.append(load_w4(1, "slot_a"))
         w1_raw.append(load_w1(1, "slot_b"))
 
-        w4s = tile("w4s", [P, 4, 4, 32], I32)
-        nc.vector.tensor_copy(
-            w4s[:].rearrange("p x t (q w) -> p x t q w", w=2),
-            w4s_raw[:].rearrange("p a (b q t w) -> p (a b) t q w", b=2, t=4, w=2),
-        )
-
+        w1q0 = [quantize("w1q0_%d" % t, w1_bf0[t][:], P) for t in range(4)]
         accs = [[bank("acc%d_%d" % (t, n), 2 * t + n, [P, NB]) for n in range(2)] for t in range(4)]
-        for a in range(2):
-            for t in range(4):
-                for n in range(2):
-                    w4_pass(accs[t][n], w4_0, 0, t, a, n)
+        for t in range(3):
+            for n in range(2):
+                for a in range(2):
+                    w4_pass(accs[t][n], w4_0, 0, t, a, n, a == 0, False)
+                w1_pass(accs[t][n], w1q0[t], n, False, True)
         for n in range(2):
-            for t in range(4):
-                w1_pass(accs[t][n], w1q0[t], n)
+            w1_pass(accs[3][n], w1q0[3], n, True, False)
+            for a in range(2):
+                w4_pass(accs[3][n], w4_0, 0, 3, a, n, False, a == 1)
         w4_1 = order_w4(1)
 
-        g2 = [tile("g2_0", [P, 4, NP], F32, "slot_a")]
+        g2 = [tile("g2_0", [P, 4, NP], F32, "slot_a2")]
         g1_0 = tile("g1_0", [P, 4, NP], F32, "slot_c")
         th = []
         accs1 = []
@@ -244,13 +247,13 @@ def tile_list_deck_synergy_chart_kernel(
             pair = [bank("acc%d_%d" % (4 + t, n), 2 * t + n, [P, NB]) for n in range(2)]
             for n in range(2):
                 for a in range(2):
-                    w4_pass(pair[n], w4_1, 1, t, a, n)
-                w1_pass(pair[n], w1q, n)
+                    w4_pass(pair[n], w4_1, 1, t, a, n, a == 0, False)
+                w1_pass(pair[n], w1q, n, False, True)
             accs1.append(pair)
             pick(g2[0][:, t, :], th[t], pos2_sb, f2[t], 0, NP)
             pick(g1_0[:, t, :], th[t], pos1_sb, f1[t], 0, NP)
 
-        g2.append(tile("g2_1", [P, 4, NP], F32, "slot_d"))
+        g2.append(tile("g2_1", [P, 4, NP], F32))
         th.append(tanh_rows(4, accs1[0]))
         pick(g2[1][:, 0, :], th[4], pos2_sb, f2[4], 0, NP)
         th.append(tanh_rows(5, accs1[1]))
@@ -295,7 +298,7 @@ def tile_list_deck_synergy_chart_kernel(
         def finish_rows(c):
             for acc, j0, j1 in e[c]:
                 res = tile("res%d_%d" % (c, j0), [P, j1 - j0], F32)
-                nc.scalar.activation(res[:], acc[:], ACT.Sigmoid, bias=coef[:, 0, 8 + c : 9 + c])
+                nc.scalar.activation(res[:], acc[:], ACT.Sigmoid, bias=base_col[:, c : c + 1])
                 nc.sync.dma_start(out[P * c : P * (c + 1), j0:j1], res[:])
 
         first = tile("g1_first", [P, 4, 2 * P], F32, "f2_7")

@@ -3,8 +3,8 @@ from contextlib import ExitStack
 import concourse.mybir as mybir
 from concourse.masks import make_identity
 
-K, KA, KB, H, T, S, NP = 1536, 1024, 512, 1024, 4096, 1024, 512
-FLOPS = 2 * K * H * S + 2 * H * NP * NP
+K, H, T, S, M = 1536, 1024, 4096, 1024, 512
+FLOPS = 2 * K * H * S + 2 * H * M * M
 
 F32 = mybir.dt.float32
 BF16 = mybir.dt.bfloat16
@@ -18,16 +18,25 @@ ACT = mybir.ActivationFunctionType
 ALU = mybir.AluOpType
 
 P = 128
-NB = 512
+BANK = 512
+HALF = 512
+SIGN_RUN = 256
+EARLY_TILES = 2
+
+KIB = 1024
 PLACES = {
-    "slot_a": 0,
-    "slot_a2": 4 * 1024,
-    "slot_aw": 15 * 1024,
-    "slot_w": 16 * 1024,
-    "slot_b": 18 * 1024,
-    "slot_bv": 29 * 1024,
-    "slot_v": 34 * 1024,
-    "slot_c": 37 * 1024,
+    "table0": 0,
+    "w4_raw1": 0,
+    "picked2_0": 4 * KIB,
+    "w4_raw0": 15 * KIB,
+    "w4_scales_raw": 16 * KIB,
+    "table1": 18 * KIB,
+    "w1_raw1": 18 * KIB,
+    "w1_raw0": 29 * KIB,
+    "v_scales": 34 * KIB,
+    "scale_windows": 37 * KIB,
+    "table2": 37 * KIB,
+    "picked1_0": 37 * KIB,
 }
 
 
@@ -38,19 +47,19 @@ def tile_list_deck_synergy_chart_kernel(
     with ExitStack() as ctx:
         lists = ctx.enter_context(tc.tile_pool(name="lists", bufs=1))
         sb = ctx.enter_context(tc.tile_pool(name="sb", bufs=1))
-        shared = ctx.enter_context(tc.tile_pool(name="shared", bufs=1))
+        reused = ctx.enter_context(tc.tile_pool(name="reused", bufs=1))
         ps = ctx.enter_context(tc.psum_pool(name="ps", bufs=1))
 
-        def tile(name, shape, dtype, tag=None):
-            if tag in PLACES:
-                return shared.tile(shape, dtype, name=name, align_bytes=64, offset=PLACES[tag])
-            return sb.tile(shape, dtype, name=name, tag=tag or name, align_bytes=64)
+        def tile(name, shape, dtype, after=None):
+            if name in PLACES:
+                return reused.tile(shape, dtype, name=name, align_bytes=64, offset=PLACES[name])
+            return sb.tile(shape, dtype, name=name, tag=after or name, align_bytes=64)
 
         def bank(name, number, shape):
             return ps.tile(shape, F32, name=name, tag="bank%d" % number)
 
-        scale_win = tile("scale_win", [P, 3, T // 4], I32, "slot_c")
-        nc.vector.memset(scale_win[:], 0)
+        scale_windows = tile("scale_windows", [P, 3, T // 4], I32)
+        nc.vector.memset(scale_windows[:], 0)
         vectors = tile("vectors", [32, H], F32)
         nc.gpsimd.memset(vectors[:], 0.0)
         rows = tile("rows", [P, 8, P], F32)
@@ -59,49 +68,48 @@ def tile_list_deck_synergy_chart_kernel(
         make_identity(nc, ident[:])
 
         offs_sb = lists.tile([P, S // 16], U16, name="offs_sb")
-        pos2_sb = lists.tile([P, NP // 16], U16, name="pos2_sb")
-        pos1_sb = lists.tile([P, NP // 16], U16, name="pos1_sb")
-        nc.sync.dma_start(offs_sb[:], offs)
+        pos2_sb = lists.tile([P, M // 16], U16, name="pos2_sb")
+        pos1_sb = lists.tile([P, M // 16], U16, name="pos1_sb")
 
-        w4_i32 = w4_words.bitcast(I32)
-        w1_rows = w1.rearrange("(p j) c -> p j c", j=4)
-
-        def load_w4(b, tag):
-            raw = tile("w4_raw%d" % b, [P, 2, 256], I32, tag)
-            nc.sync.dma_start(raw[:], w4_i32[:, :, 256 * b : 256 * (b + 1)].rearrange("a p w -> p a w"))
+        def load_w4(b):
+            raw = tile("w4_raw%d" % b, [P, 2, HALF // 2], I32)
+            half = w4_words.bitcast(I32)[:, :, HALF // 2 * b : HALF // 2 * (b + 1)]
+            nc.sync.dma_start(raw[:], half.rearrange("a p w -> p a w"))
             return raw
 
-        def load_w1(b, tag):
-            raw = tile("w1_raw%d" % b, [P, 4, NB], F32, tag)
-            nc.sync.dma_start(raw[:], w1_rows[:, :, NB * b : NB * (b + 1)])
+        def load_w1(b):
+            raw = tile("w1_raw%d" % b, [P, 4, HALF], F32)
+            nc.sync.dma_start(raw[:], w1.rearrange("(p j) c -> p j c", j=4)[:, :, HALF * b : HALF * (b + 1)])
             return raw
 
-        def load_table(a, tag):
-            words = tile("table%d" % a, [P, T], I32, tag)
+        def load_table(a):
+            words = tile("table%d" % a, [P, T], I32)
             nc.sync.dma_start(words[:], tab_words[a].rearrange("p t i -> p (t i)").bitcast(I32))
             return words
 
+        nc.sync.dma_start(offs_sb[:], offs)
         nc.sync.dma_start(pos2_sb[:], pos2)
         nc.sync.dma_start(pos1_sb[:], pos1)
-        w4_raw = [load_w4(0, "slot_aw")]
-        w1_raw = [load_w1(0, "slot_bv")]
-        nc.sync.dma_start(scale_win[0:P:8, :, :], tab_scales.bitcast(I32).rearrange("a q w -> q a w"))
+        w4_raw = [load_w4(0)]
+        w1_raw = [load_w1(0)]
+        nc.sync.dma_start(scale_windows[0:P:8, :, :], tab_scales.bitcast(I32).rearrange("a q w -> q a w"))
         nc.scalar.dma_start(vectors[0:1, :], gain.rearrange("(o r) -> o r", o=1))
         nc.scalar.dma_start(vectors[1:2, :], pay.rearrange("(o r) -> o r", o=1))
         nc.scalar.dma_start(rows[32:36, 0, :], base.rearrange("(c p) -> c p", p=P))
+
         def order_w4(b):
-            dst = tile("w4_%d" % b, [P, 2, 4, 64], I32)
+            dst = tile("w4_%d" % b, [P, 2, 4, P // 2], I32)
             nc.vector.tensor_copy(
                 dst[:].rearrange("p a t (q w) -> p a t q w", w=4),
                 w4_raw[b][:].rearrange("p a (q t w) -> p a t q w", t=4, w=4),
             )
             return dst
 
-        def round_w1(b, t, tag):
-            dst = tile("w1_bf%d_%d" % (b, t), [P, P * 4], BF16, tag)
+        def round_w1(b, t, after=None):
+            dst = tile("w1_bf%d_%d" % (b, t), [P, P * 4], BF16, after)
             nc.scalar.copy(
-                dst[:].rearrange("p (q h l j) -> p q h j l", h=2, l=4, j=4),
-                w1_raw[b][:].rearrange("p j (q t h l) -> p t q h j l", t=4, h=2, l=4)[:, t],
+                dst[:].rearrange("p (q g l j) -> p q g j l", g=2, l=4, j=4),
+                w1_raw[b][:].rearrange("p j (q t g l) -> p t q g j l", t=4, g=2, l=4)[:, t],
             )
             return dst
 
@@ -112,38 +120,38 @@ def tile_list_deck_synergy_chart_kernel(
             return codes, scales
 
         def w4_pass(acc, w4_b, b, t, a, n, start, stop):
-            cols = slice(NB * n, NB * (n + 1))
+            cols = slice(BANK * n, BANK * (n + 1))
             nc.tensor.matmul_mx(
                 out=acc[:],
                 lhsT=w4_b[:, a, t, :].bitcast(FP4X4),
-                lhsT_scale=w4s[:, 2 * a + b, t, :].bitcast(U8),
+                lhsT_scale=w4_scales_sb[:, 2 * a + b, t, :].bitcast(U8),
                 rhs=v_words[a][:, cols].bitcast(FP8X4),
                 rhs_scale=v_scales[:, a, :].bitcast(U8)[:, cols],
                 start=start,
                 stop=stop,
             )
 
-        def w1_pass(acc, w1q, n, start, stop):
-            cols = slice(NB * n, NB * (n + 1))
+        def w1_pass(acc, w1_q, n, start, stop):
+            cols = slice(BANK * n, BANK * (n + 1))
             nc.tensor.matmul_mx(
                 out=acc[:],
-                lhsT=w1q[0][:].bitcast(FP8X4),
-                lhsT_scale=w1q[1][:],
+                lhsT=w1_q[0][:].bitcast(FP8X4),
+                lhsT_scale=w1_q[1][:],
                 rhs=v_words[2][:, cols].bitcast(FP8X4),
                 rhs_scale=v_scales[:, 2, :].bitcast(U8)[:, cols],
                 start=start,
                 stop=stop,
             )
 
-        def tanh_rows(s, accs):
-            th = tile("tanh%d" % s, [P, S], F32)
+        def tanh_rows(s, sums):
+            window = tile("tanh%d" % s, [P, S], F32)
             for n in range(2):
-                nc.scalar.activation(th[:, NB * n : NB * (n + 1)], accs[n][:], ACT.Tanh)
-            return th
+                nc.scalar.activation(window[:, BANK * n : BANK * (n + 1)], sums[n][:], ACT.Tanh)
+            return window
 
-        def pick(dst, th, pos_sb, factor, m0, m1):
+        def pick(dst, window, pos_sb, factor, m0, m1):
             nc.vector.tensor_tensor(
-                dst, th[:].indirect(pos_sb[:, m0 // 16 : m1 // 16]), factor[:, 0 : m1 - m0], ALU.mult
+                dst, window[:].indirect(pos_sb[:, m0 // 16 : m1 // 16]), factor[:, 0 : m1 - m0], ALU.mult
             )
 
         def weave(dst, src, func):
@@ -153,172 +161,174 @@ def tile_list_deck_synergy_chart_kernel(
 
         def apply_sign(dst, src, b):
             nc.vector.tensor_tensor(
-                dst.rearrange("p (x y) -> p x y", y=256),
-                src.rearrange("p (x y) -> p x y", y=256),
-                signs[:, b].rearrange("p c t -> p (c t)").unsqueeze(1).to_broadcast([P, NP * 4 // 256, 256]),
+                dst.rearrange("p (x y) -> p x y", y=SIGN_RUN),
+                src.rearrange("p (x y) -> p x y", y=SIGN_RUN),
+                signs[:, b].rearrange("p c t -> p (c t)").unsqueeze(1).to_broadcast([P, M * 4 // SIGN_RUN, SIGN_RUN]),
                 ALU.mult,
             )
 
         w4_0 = order_w4(0)
-        table = [load_table(0, "slot_a")]
-        w4s_raw = tile("w4s_raw", [P, 2, H // 4], I32, "slot_w")
-        nc.gpsimd.memset(w4s_raw[:], 0)
-        w4s_i32 = w4_scales.bitcast(I32)
-        for r in range(4):
-            nc.scalar.dma_start(w4s_raw[r:P:32, :, :], w4s_i32[:, r:16:4, :].rearrange("a q w -> q a w"))
+        table = [load_table(0)]
+        w4_scales_raw = tile("w4_scales_raw", [P, 2, H // 4], I32)
+        nc.gpsimd.memset(w4_scales_raw[:], 0)
+        for u in range(4):
+            nc.scalar.dma_start(
+                w4_scales_raw[u:P:32, :, :], w4_scales.bitcast(I32)[:, u:16:4, :].rearrange("a q w -> q a w")
+            )
+        w1_bf0 = [round_w1(0, t) for t in range(4)]
 
-        w1_bf0 = [round_w1(0, t, None) for t in range(4)]
-
-        nc.scalar.copy(
+        nc.vector.tensor_copy(
             rows[0:32].rearrange("v (b t) (q i) -> v b t q i", t=4, i=8),
             vectors[:].rearrange("v (b q t i) -> v b t q i", b=2, t=4, i=8),
         )
-        coef = tile("coef", [P, 2, 4, 2], F32)
+        gain_pay = tile("gain_pay", [P, 2, 4, 2], F32)
         base_col = tile("base_col", [P, 4], F32)
         for b in range(2):
             rows_t = bank("rows_t%d" % b, 6 + b, [P, 4, P])
             for t in range(4):
                 nc.tensor.transpose(rows_t[:, t, :], rows[:, 4 * b + t, :], ident[:])
-            nc.scalar.copy(coef[:, b], rows_t[:, :, 0:2])
+            nc.scalar.copy(gain_pay[:, b], rows_t[:, :, 0:2])
             if b == 0:
                 nc.scalar.copy(base_col[:], rows_t[:, 0, 32:36])
-        table.append(load_table(1, "slot_b"))
-        v_scales = tile("v_scales", [P, 3, S // 4], I32, "slot_v")
+        table.append(load_table(1))
+        v_scales = tile("v_scales", [P, 3, S // 4], I32)
         nc.gpsimd.memset(v_scales[:], 0)
 
-        f1 = []
-        f2 = []
-
+        factor1 = []
+        factor2 = []
         for s in range(8):
             b, t = divmod(s, 4)
-            f1_s = tile("f1_%d" % s, [P, NP], F32)
-            nc.scalar.copy(f1_s[:], coef[:, b, t, 0:1].to_broadcast([P, NP]))
-            f2_s = tile("f2_%d" % s, [P, NP], F32)
-            nc.scalar.activation(f2_s[:], f1_s[:], ACT.Copy, scale=coef[:, b, t, 1:2])
-            f1.append(f1_s)
-            f2.append(f2_s)
-        signs = tile("signs", [P, 2, 64, 4], BF16)
-        nc.scalar.activation(signs[:], coef[:, :, :, 1].unsqueeze(2).to_broadcast([P, 2, 64, 4]), ACT.Sign)
+            gain_s = tile("factor1_%d" % s, [P, M], F32)
+            nc.scalar.copy(gain_s[:], gain_pay[:, b, t, 0:1].to_broadcast([P, M]))
+            both_s = tile("factor2_%d" % s, [P, M], F32)
+            nc.scalar.activation(both_s[:], gain_s[:], ACT.Copy, scale=gain_pay[:, b, t, 1:2])
+            factor1.append(gain_s)
+            factor2.append(both_s)
+        signs = tile("signs", [P, 2, SIGN_RUN // 4, 4], BF16)
+        nc.scalar.activation(
+            signs[:], gain_pay[:, :, :, 1].unsqueeze(2).to_broadcast([P, 2, SIGN_RUN // 4, 4]), ACT.Sign
+        )
 
         picked_scales = tile("picked_scales", [P, 3, S], U8)
         for a in range(3):
-            nc.vector.tensor_copy(picked_scales[:, a, :], scale_win[:, a, :].bitcast(U8).indirect(offs_sb[:]))
-        for r in range(4):
-            nc.sync.dma_start(v_scales[r:P:32, :, :], picked_scales[8 * r : P : 32, :, :].bitcast(I32))
-        table.append(load_table(2, "slot_c"))
-        w4s = tile("w4s", [P, 4, 4, 32], I32)
+            nc.vector.tensor_copy(picked_scales[:, a, :], scale_windows[:, a, :].bitcast(U8).indirect(offs_sb[:]))
+        for u in range(4):
+            nc.sync.dma_start(v_scales[u:P:32, :, :], picked_scales[8 * u : P : 32, :, :].bitcast(I32))
+        table.append(load_table(2))
+        w4_scales_sb = tile("w4_scales_sb", [P, 4, 4, P // 4], I32)
         nc.vector.tensor_copy(
-            w4s[:].rearrange("p x t (q w) -> p x t q w", w=2),
-            w4s_raw[:].rearrange("p a (b q t w) -> p (a b) t q w", b=2, t=4, w=2),
+            w4_scales_sb[:].rearrange("p x t (q w) -> p x t q w", w=2),
+            w4_scales_raw[:].rearrange("p a (b q t w) -> p (a b) t q w", b=2, t=4, w=2),
         )
-
         v_words = []
         for a in range(3):
             v_a = tile("v_words%d" % a, [P, S], U32)
-            step = NB if a == 2 else S
+            step = BANK if a == 2 else S
             for j in range(0, S, step):
                 nc.vector.tensor_copy(
                     v_a[:, j : j + step], table[a][:].bitcast(U32).indirect(offs_sb[:, j // 16 : (j + step) // 16])
                 )
             v_words.append(v_a)
-        w4_raw.append(load_w4(1, "slot_a"))
-        w1_raw.append(load_w1(1, "slot_b"))
+        w4_raw.append(load_w4(1))
+        w1_raw.append(load_w1(1))
 
-        w1q0 = [quantize("w1q0_%d" % t, w1_bf0[t][:], P) for t in range(4)]
-        accs = [[bank("acc%d_%d" % (t, n), 2 * t + n, [P, NB]) for n in range(2)] for t in range(4)]
-        for t in range(3):
+        w1_q0 = [quantize("w1_q0_%d" % t, w1_bf0[t][:], P) for t in range(4)]
+        sums0 = [[bank("sum%d_%d" % (t, n), 2 * t + n, [P, BANK]) for n in range(2)] for t in range(4)]
+        for t in range(EARLY_TILES):
             for n in range(2):
                 for a in range(2):
-                    w4_pass(accs[t][n], w4_0, 0, t, a, n, a == 0, False)
-                w1_pass(accs[t][n], w1q0[t], n, False, True)
-        for n in range(2):
-            w1_pass(accs[3][n], w1q0[3], n, True, False)
-            for a in range(2):
-                w4_pass(accs[3][n], w4_0, 0, 3, a, n, False, a == 1)
+                    w4_pass(sums0[t][n], w4_0, 0, t, a, n, a == 0, False)
+                w1_pass(sums0[t][n], w1_q0[t], n, False, True)
+        for t in range(EARLY_TILES, 4):
+            for n in range(2):
+                w1_pass(sums0[t][n], w1_q0[t], n, True, False)
+                for a in range(2):
+                    w4_pass(sums0[t][n], w4_0, 0, t, a, n, False, a == 1)
         w4_1 = order_w4(1)
 
-        g2 = [tile("g2_0", [P, 4, NP], F32, "slot_a2")]
-        g1_0 = tile("g1_0", [P, 4, NP], F32, "slot_c")
-        th = []
-        accs1 = []
+        picked2 = [tile("picked2_0", [P, 4, M], F32)]
+        picked1_0 = tile("picked1_0", [P, 4, M], F32)
+        windows = []
+        sums1 = []
         for t in range(4):
-            th.append(tanh_rows(t, accs[t]))
-            w1q = quantize("w1q1_%d" % t, round_w1(1, t, "w1q0_%d_codes" % t)[:], P)
-            pair = [bank("acc%d_%d" % (4 + t, n), 2 * t + n, [P, NB]) for n in range(2)]
+            windows.append(tanh_rows(t, sums0[t]))
+            w1_q = quantize("w1_q1_%d" % t, round_w1(1, t, "w1_q0_%d_codes" % t)[:], P)
+            pair = [bank("sum%d_%d" % (4 + t, n), 2 * t + n, [P, BANK]) for n in range(2)]
             for n in range(2):
                 for a in range(2):
                     w4_pass(pair[n], w4_1, 1, t, a, n, a == 0, False)
-                w1_pass(pair[n], w1q, n, False, True)
-            accs1.append(pair)
-            pick(g2[0][:, t, :], th[t], pos2_sb, f2[t], 0, NP)
-            pick(g1_0[:, t, :], th[t], pos1_sb, f1[t], 0, NP)
+                w1_pass(pair[n], w1_q, n, False, True)
+            sums1.append(pair)
+            pick(picked2[0][:, t, :], windows[t], pos2_sb, factor2[t], 0, M)
+            pick(picked1_0[:, t, :], windows[t], pos1_sb, factor1[t], 0, M)
 
-        g2.append(tile("g2_1", [P, 4, NP], F32))
-        th.append(tanh_rows(4, accs1[0]))
-        pick(g2[1][:, 0, :], th[4], pos2_sb, f2[4], 0, NP)
-        th.append(tanh_rows(5, accs1[1]))
-        pick(g2[1][:, 1, :], th[5], pos2_sb, f2[5], 0, NP)
-        x2_0 = tile("x2_0", [P, NP * 4], BF16)
-        weave(x2_0[:], g2[0][:], ACT.Abs)
-        th.append(tanh_rows(6, accs1[2]))
-        pick(g2[1][:, 2, :], th[6], pos2_sb, f2[6], 0, NP)
-        th.append(tanh_rows(7, accs1[3]))
-        pick(g2[1][:, 3, :], th[7], pos2_sb, f2[7], 0, NP)
+        picked2.append(tile("picked2_1", [P, 4, M], F32))
+
+        def tanh_and_pick2(t):
+            windows.append(tanh_rows(4 + t, sums1[t]))
+            pick(picked2[1][:, t, :], windows[4 + t], pos2_sb, factor2[4 + t], 0, M)
+
+        for t in range(2):
+            tanh_and_pick2(t)
+        x2_0 = tile("x2_0", [P, M * 4], BF16)
+        weave(x2_0[:], picked2[0][:], ACT.Abs)
+        for t in range(2, 4):
+            tanh_and_pick2(t)
         apply_sign(x2_0[:], x2_0[:], 0)
-        x2q = [quantize("x2q0", x2_0[:], NP)]
-        x1_0 = tile("x1_0", [P, NP * 4], BF16)
-        weave(x1_0[:], g1_0[:], ACT.Copy)
-        x1q0 = quantize("x1q0", x1_0[:], NP)
+        x2_q = [quantize("x2_q0", x2_0[:], M)]
+        x1_0 = tile("x1_0", [P, M * 4], BF16)
+        weave(x1_0[:], picked1_0[:], ACT.Copy)
+        x1_q0 = quantize("x1_q0", x1_0[:], M)
 
-        def product_pass(acc, x1q, cols, x2q_b, j0, j1, first_pass):
+        def product_pass(acc, x1_q, cols, x2_q_b, j0, j1, first_pass):
             nc.tensor.matmul_mx(
                 out=acc[:],
-                lhsT=x1q[0][:, cols].bitcast(FP8X4),
-                lhsT_scale=x1q[1][:, cols],
-                rhs=x2q_b[0][:, j0:j1].bitcast(FP8X4),
-                rhs_scale=x2q_b[1][:, j0:j1],
+                lhsT=x1_q[0][:, cols].bitcast(FP8X4),
+                lhsT_scale=x1_q[1][:, cols],
+                rhs=x2_q_b[0][:, j0:j1].bitcast(FP8X4),
+                rhs_scale=x2_q_b[1][:, j0:j1],
                 start=first_pass,
                 stop=not first_pass,
             )
 
-        e = [[(bank("e%d" % c, c, [P, NP]), 0, NP)] for c in range(3)]
-        e.append([(bank("e3_%d" % h, 3 + h, [P, NP // 2]), NP // 2 * h, NP // 2 * (h + 1)) for h in range(2)])
+        scores = [[(bank("score%d" % c, c, [P, M]), 0, M)] for c in range(3)]
+        scores.append([(bank("score3_%d" % n, 3 + n, [P, M // 2]), M // 2 * n, M // 2 * (n + 1)) for n in range(2)])
         for c in range(4):
-            for acc, j0, j1 in e[c]:
-                product_pass(acc, x1q0, slice(P * c, P * (c + 1)), x2q[0], j0, j1, True)
+            for acc, j0, j1 in scores[c]:
+                product_pass(acc, x1_q0, slice(P * c, P * (c + 1)), x2_q[0], j0, j1, True)
 
-        x2_abs = tile("x2_abs", [P, NP * 4], BF16)
-        x2_1 = tile("x2_1", [P, NP * 4], BF16)
-        weave(x2_abs[:], g2[1][:], ACT.Abs)
+        x2_abs = tile("x2_abs", [P, M * 4], BF16)
+        x2_1 = tile("x2_1", [P, M * 4], BF16)
+        weave(x2_abs[:], picked2[1][:], ACT.Abs)
 
-        def finish_product(c, x1q, cols):
-            for acc, j0, j1 in e[c]:
-                product_pass(acc, x1q, cols, x2q[1], j0, j1, False)
+        def finish_product(c, x1_q, cols):
+            for acc, j0, j1 in scores[c]:
+                product_pass(acc, x1_q, cols, x2_q[1], j0, j1, False)
 
         def finish_rows(c):
-            for acc, j0, j1 in e[c]:
-                res = tile("res%d_%d" % (c, j0), [P, j1 - j0], F32)
-                nc.scalar.activation(res[:], acc[:], ACT.Sigmoid, bias=base_col[:, c : c + 1])
-                nc.sync.dma_start(out[P * c : P * (c + 1), j0:j1], res[:])
+            for acc, j0, j1 in scores[c]:
+                result = tile("result%d_%d" % (c, j0), [P, j1 - j0], F32)
+                nc.scalar.activation(result[:], acc[:], ACT.Sigmoid, bias=base_col[:, c : c + 1])
+                nc.sync.dma_start(out[P * c : P * (c + 1), j0:j1], result[:])
 
-        first = tile("g1_first", [P, 4, 2 * P], F32, "f2_7")
+        first = tile("picked1_first", [P, 4, 2 * P], F32, "factor2_7")
         for t in range(4):
-            pick(first[:, t, :], th[4 + t], pos1_sb, f1[4 + t], 0, 2 * P)
+            pick(first[:, t, :], windows[4 + t], pos1_sb, factor1[4 + t], 0, 2 * P)
         apply_sign(x2_1[:], x2_abs[:], 1)
-        x2q.append(quantize("x2q1", x2_1[:], NP))
+        x2_q.append(quantize("x2_q1", x2_1[:], M))
         x1_first = tile("x1_first", [P, 2 * P * 4], BF16)
         weave(x1_first[:], first[:], ACT.Copy)
-        x1q_first = quantize("x1q_first", x1_first[:], 2 * P)
+        x1_q_first = quantize("x1_q_first", x1_first[:], 2 * P)
         for c in range(2):
-            finish_product(c, x1q_first, slice(P * c, P * (c + 1)))
+            finish_product(c, x1_q_first, slice(P * c, P * (c + 1)))
 
-        rest = tile("g1_rest", [P, 2, 4, P], F32, "x2_abs")
-        for c, tag in ((2, "x1q_first_codes"), (3, "x1q_first_scales")):
+        rest = tile("picked1_rest", [P, 2, 4, P], F32, "x2_abs")
+        for c, after in ((2, "x1_q_first_codes"), (3, "x1_q_first_scales")):
             finish_rows(c - 2)
             for t in range(4):
-                pick(rest[:, c - 2, t, :], th[4 + t], pos1_sb, f1[4 + t], P * c, P * (c + 1))
-            x1_c = tile("x1_rest%d" % c, [P, P * 4], BF16, tag)
+                pick(rest[:, c - 2, t, :], windows[4 + t], pos1_sb, factor1[4 + t], P * c, P * (c + 1))
+            x1_c = tile("x1_rest%d" % c, [P, P * 4], BF16, after)
             weave(x1_c[:], rest[:, c - 2], ACT.Copy)
-            finish_product(c, quantize("x1q_rest%d" % c, x1_c[:], P), slice(0, P))
+            finish_product(c, quantize("x1_q_rest%d" % c, x1_c[:], P), slice(0, P))
         for c in range(2, 4):
             finish_rows(c)

from contextlib import ExitStack

import concourse.mybir as mybir
from concourse.masks import make_identity

K, H, T, S, M = 1536, 1024, 4096, 1024, 512
FLOPS = 2 * K * H * S + 2 * H * M * M

F32 = mybir.dt.float32
BF16 = mybir.dt.bfloat16
I32 = mybir.dt.int32
U32 = mybir.dt.uint32
U16 = mybir.dt.uint16
U8 = mybir.dt.uint8
FP8X4 = mybir.dt.float8_e4m3fn_x4
FP4X4 = mybir.dt.float4_e2m1fn_x4
ACT = mybir.ActivationFunctionType
ALU = mybir.AluOpType

P = 128
BANK = 512
HALF = 512
SIGN_RUN = 256
EARLY_TILES = 2

KIB = 1024
PLACES = {
    "table0": 0,
    "w4_raw1": 0,
    "picked2_0": 4 * KIB,
    "w4_raw0": 15 * KIB,
    "w4_scales_raw": 16 * KIB,
    "table1": 18 * KIB,
    "w1_raw1": 18 * KIB,
    "w1_raw0": 29 * KIB,
    "v_scales": 34 * KIB,
    "scale_windows": 37 * KIB,
    "table2": 37 * KIB,
    "picked1_0": 37 * KIB,
}


def tile_list_deck_synergy_chart_kernel(
    tc, tab_words, tab_scales, offs, w4_words, w4_scales, w1, gain, pos1, pos2, pay, base, out
):
    nc = tc.nc
    with ExitStack() as ctx:
        lists = ctx.enter_context(tc.tile_pool(name="lists", bufs=1))
        sb = ctx.enter_context(tc.tile_pool(name="sb", bufs=1))
        reused = ctx.enter_context(tc.tile_pool(name="reused", bufs=1))
        ps = ctx.enter_context(tc.psum_pool(name="ps", bufs=1))

        def tile(name, shape, dtype, after=None):
            if name in PLACES:
                return reused.tile(shape, dtype, name=name, align_bytes=64, offset=PLACES[name])
            return sb.tile(shape, dtype, name=name, tag=after or name, align_bytes=64)

        def bank(name, number, shape):
            return ps.tile(shape, F32, name=name, tag="bank%d" % number)

        scale_windows = tile("scale_windows", [P, 3, T // 4], I32)
        nc.vector.memset(scale_windows[:], 0)
        vectors = tile("vectors", [32, H], F32)
        nc.gpsimd.memset(vectors[:], 0.0)
        rows = tile("rows", [P, 8, P], F32)
        nc.gpsimd.memset(rows[:], 0.0)
        ident = tile("ident", [P, P], F32)
        make_identity(nc, ident[:])

        offs_sb = lists.tile([P, S // 16], U16, name="offs_sb")
        pos2_sb = lists.tile([P, M // 16], U16, name="pos2_sb")
        pos1_sb = lists.tile([P, M // 16], U16, name="pos1_sb")

        def load_w4(b):
            raw = tile("w4_raw%d" % b, [P, 2, HALF // 2], I32)
            half = w4_words.bitcast(I32)[:, :, HALF // 2 * b : HALF // 2 * (b + 1)]
            nc.sync.dma_start(raw[:], half.rearrange("a p w -> p a w"))
            return raw

        def load_w1(b):
            raw = tile("w1_raw%d" % b, [P, 4, HALF], F32)
            nc.sync.dma_start(raw[:], w1.rearrange("(p j) c -> p j c", j=4)[:, :, HALF * b : HALF * (b + 1)])
            return raw

        def load_table(a):
            words = tile("table%d" % a, [P, T], I32)
            nc.sync.dma_start(words[:], tab_words[a].rearrange("p t i -> p (t i)").bitcast(I32))
            return words

        nc.sync.dma_start(offs_sb[:], offs)
        nc.sync.dma_start(pos2_sb[:], pos2)
        nc.sync.dma_start(pos1_sb[:], pos1)
        w4_raw = [load_w4(0)]
        w1_raw = [load_w1(0)]
        nc.sync.dma_start(scale_windows[0:P:8, :, :], tab_scales.bitcast(I32).rearrange("a q w -> q a w"))
        nc.scalar.dma_start(vectors[0:1, :], gain.rearrange("(o r) -> o r", o=1))
        nc.scalar.dma_start(vectors[1:2, :], pay.rearrange("(o r) -> o r", o=1))
        nc.scalar.dma_start(rows[32:36, 0, :], base.rearrange("(c p) -> c p", p=P))

        def order_w4(b):
            dst = tile("w4_%d" % b, [P, 2, 4, P // 2], I32)
            nc.vector.tensor_copy(
                dst[:].rearrange("p a t (q w) -> p a t q w", w=4),
                w4_raw[b][:].rearrange("p a (q t w) -> p a t q w", t=4, w=4),
            )
            return dst

        def round_w1(b, t, after=None):
            dst = tile("w1_bf%d_%d" % (b, t), [P, P * 4], BF16, after)
            nc.scalar.copy(
                dst[:].rearrange("p (q g l j) -> p q g j l", g=2, l=4, j=4),
                w1_raw[b][:].rearrange("p j (q t g l) -> p t q g j l", t=4, g=2, l=4)[:, t],
            )
            return dst

        def quantize(name, src, width):
            codes = tile(name + "_codes", [P, width], U32)
            scales = tile(name + "_scales", [P, width], U8)
            nc.vector.quantize_mx(out=codes[:].bitcast(FP8X4), scales=scales[:], in_=src)
            return codes, scales

        def w4_pass(acc, w4_b, b, t, a, n, start, stop):
            cols = slice(BANK * n, BANK * (n + 1))
            nc.tensor.matmul_mx(
                out=acc[:],
                lhsT=w4_b[:, a, t, :].bitcast(FP4X4),
                lhsT_scale=w4_scales_sb[:, 2 * a + b, t, :].bitcast(U8),
                rhs=v_words[a][:, cols].bitcast(FP8X4),
                rhs_scale=v_scales[:, a, :].bitcast(U8)[:, cols],
                start=start,
                stop=stop,
            )

        def w1_pass(acc, w1_q, n, start, stop):
            cols = slice(BANK * n, BANK * (n + 1))
            nc.tensor.matmul_mx(
                out=acc[:],
                lhsT=w1_q[0][:].bitcast(FP8X4),
                lhsT_scale=w1_q[1][:],
                rhs=v_words[2][:, cols].bitcast(FP8X4),
                rhs_scale=v_scales[:, 2, :].bitcast(U8)[:, cols],
                start=start,
                stop=stop,
            )

        def tanh_rows(s, sums):
            window = tile("tanh%d" % s, [P, S], F32)
            for n in range(2):
                nc.scalar.activation(window[:, BANK * n : BANK * (n + 1)], sums[n][:], ACT.Tanh)
            return window

        def pick(dst, window, pos_sb, factor, m0, m1):
            nc.vector.tensor_tensor(
                dst, window[:].indirect(pos_sb[:, m0 // 16 : m1 // 16]), factor[:, 0 : m1 - m0], ALU.mult
            )

        def weave(dst, src, func):
            nc.scalar.activation(
                dst.rearrange("p (c i t) -> p c t i", i=4, t=4), src.rearrange("p t (c i) -> p c t i", i=4), func
            )

        def apply_sign(dst, src, b):
            nc.vector.tensor_tensor(
                dst.rearrange("p (x y) -> p x y", y=SIGN_RUN),
                src.rearrange("p (x y) -> p x y", y=SIGN_RUN),
                signs[:, b].rearrange("p c t -> p (c t)").unsqueeze(1).to_broadcast([P, M * 4 // SIGN_RUN, SIGN_RUN]),
                ALU.mult,
            )

        w4_0 = order_w4(0)
        table = [load_table(0)]
        w4_scales_raw = tile("w4_scales_raw", [P, 2, H // 4], I32)
        nc.gpsimd.memset(w4_scales_raw[:], 0)
        for u in range(4):
            nc.scalar.dma_start(
                w4_scales_raw[u:P:32, :, :], w4_scales.bitcast(I32)[:, u:16:4, :].rearrange("a q w -> q a w")
            )
        w1_bf0 = [round_w1(0, t) for t in range(4)]

        nc.vector.tensor_copy(
            rows[0:32].rearrange("v (b t) (q i) -> v b t q i", t=4, i=8),
            vectors[:].rearrange("v (b q t i) -> v b t q i", b=2, t=4, i=8),
        )
        gain_pay = tile("gain_pay", [P, 2, 4, 2], F32)
        base_col = tile("base_col", [P, 4], F32)
        for b in range(2):
            rows_t = bank("rows_t%d" % b, 6 + b, [P, 4, P])
            for t in range(4):
                nc.tensor.transpose(rows_t[:, t, :], rows[:, 4 * b + t, :], ident[:])
            nc.scalar.copy(gain_pay[:, b], rows_t[:, :, 0:2])
            if b == 0:
                nc.scalar.copy(base_col[:], rows_t[:, 0, 32:36])
        table.append(load_table(1))
        v_scales = tile("v_scales", [P, 3, S // 4], I32)
        nc.gpsimd.memset(v_scales[:], 0)

        factor1 = []
        factor2 = []
        for s in range(8):
            b, t = divmod(s, 4)
            gain_s = tile("factor1_%d" % s, [P, M], F32)
            nc.scalar.copy(gain_s[:], gain_pay[:, b, t, 0:1].to_broadcast([P, M]))
            both_s = tile("factor2_%d" % s, [P, M], F32)
            nc.scalar.activation(both_s[:], gain_s[:], ACT.Copy, scale=gain_pay[:, b, t, 1:2])
            factor1.append(gain_s)
            factor2.append(both_s)
        signs = tile("signs", [P, 2, SIGN_RUN // 4, 4], BF16)
        nc.scalar.activation(
            signs[:], gain_pay[:, :, :, 1].unsqueeze(2).to_broadcast([P, 2, SIGN_RUN // 4, 4]), ACT.Sign
        )

        picked_scales = tile("picked_scales", [P, 3, S], U8)
        for a in range(3):
            nc.vector.tensor_copy(picked_scales[:, a, :], scale_windows[:, a, :].bitcast(U8).indirect(offs_sb[:]))
        for u in range(4):
            nc.sync.dma_start(v_scales[u:P:32, :, :], picked_scales[8 * u : P : 32, :, :].bitcast(I32))
        table.append(load_table(2))
        w4_scales_sb = tile("w4_scales_sb", [P, 4, 4, P // 4], I32)
        nc.vector.tensor_copy(
            w4_scales_sb[:].rearrange("p x t (q w) -> p x t q w", w=2),
            w4_scales_raw[:].rearrange("p a (b q t w) -> p (a b) t q w", b=2, t=4, w=2),
        )
        v_words = []
        for a in range(3):
            v_a = tile("v_words%d" % a, [P, S], U32)
            step = BANK if a == 2 else S
            for j in range(0, S, step):
                nc.vector.tensor_copy(
                    v_a[:, j : j + step], table[a][:].bitcast(U32).indirect(offs_sb[:, j // 16 : (j + step) // 16])
                )
            v_words.append(v_a)
        w4_raw.append(load_w4(1))
        w1_raw.append(load_w1(1))

        w1_q0 = [quantize("w1_q0_%d" % t, w1_bf0[t][:], P) for t in range(4)]
        sums0 = [[bank("sum%d_%d" % (t, n), 2 * t + n, [P, BANK]) for n in range(2)] for t in range(4)]
        for t in range(EARLY_TILES):
            for n in range(2):
                for a in range(2):
                    w4_pass(sums0[t][n], w4_0, 0, t, a, n, a == 0, False)
                w1_pass(sums0[t][n], w1_q0[t], n, False, True)
        for t in range(EARLY_TILES, 4):
            for n in range(2):
                w1_pass(sums0[t][n], w1_q0[t], n, True, False)
                for a in range(2):
                    w4_pass(sums0[t][n], w4_0, 0, t, a, n, False, a == 1)
        w4_1 = order_w4(1)

        picked2 = [tile("picked2_0", [P, 4, M], F32)]
        picked1_0 = tile("picked1_0", [P, 4, M], F32)
        windows = []
        sums1 = []
        for t in range(4):
            windows.append(tanh_rows(t, sums0[t]))
            w1_q = quantize("w1_q1_%d" % t, round_w1(1, t, "w1_q0_%d_codes" % t)[:], P)
            pair = [bank("sum%d_%d" % (4 + t, n), 2 * t + n, [P, BANK]) for n in range(2)]
            for n in range(2):
                for a in range(2):
                    w4_pass(pair[n], w4_1, 1, t, a, n, a == 0, False)
                w1_pass(pair[n], w1_q, n, False, True)
            sums1.append(pair)
            pick(picked2[0][:, t, :], windows[t], pos2_sb, factor2[t], 0, M)
            pick(picked1_0[:, t, :], windows[t], pos1_sb, factor1[t], 0, M)

        picked2.append(tile("picked2_1", [P, 4, M], F32))

        def tanh_and_pick2(t):
            windows.append(tanh_rows(4 + t, sums1[t]))
            pick(picked2[1][:, t, :], windows[4 + t], pos2_sb, factor2[4 + t], 0, M)

        for t in range(2):
            tanh_and_pick2(t)
        x2_0 = tile("x2_0", [P, M * 4], BF16)
        weave(x2_0[:], picked2[0][:], ACT.Abs)
        for t in range(2, 4):
            tanh_and_pick2(t)
        apply_sign(x2_0[:], x2_0[:], 0)
        x2_q = [quantize("x2_q0", x2_0[:], M)]
        x1_0 = tile("x1_0", [P, M * 4], BF16)
        weave(x1_0[:], picked1_0[:], ACT.Copy)
        x1_q0 = quantize("x1_q0", x1_0[:], M)

        def product_pass(acc, x1_q, cols, x2_q_b, j0, j1, first_pass):
            nc.tensor.matmul_mx(
                out=acc[:],
                lhsT=x1_q[0][:, cols].bitcast(FP8X4),
                lhsT_scale=x1_q[1][:, cols],
                rhs=x2_q_b[0][:, j0:j1].bitcast(FP8X4),
                rhs_scale=x2_q_b[1][:, j0:j1],
                start=first_pass,
                stop=not first_pass,
            )

        scores = [[(bank("score%d" % c, c, [P, M]), 0, M)] for c in range(3)]
        scores.append([(bank("score3_%d" % n, 3 + n, [P, M // 2]), M // 2 * n, M // 2 * (n + 1)) for n in range(2)])
        for c in range(4):
            for acc, j0, j1 in scores[c]:
                product_pass(acc, x1_q0, slice(P * c, P * (c + 1)), x2_q[0], j0, j1, True)

        x2_abs = tile("x2_abs", [P, M * 4], BF16)
        x2_1 = tile("x2_1", [P, M * 4], BF16)
        weave(x2_abs[:], picked2[1][:], ACT.Abs)

        def finish_product(c, x1_q, cols):
            for acc, j0, j1 in scores[c]:
                product_pass(acc, x1_q, cols, x2_q[1], j0, j1, False)

        def finish_rows(c):
            for acc, j0, j1 in scores[c]:
                result = tile("result%d_%d" % (c, j0), [P, j1 - j0], F32)
                nc.scalar.activation(result[:], acc[:], ACT.Sigmoid, bias=base_col[:, c : c + 1])
                nc.sync.dma_start(out[P * c : P * (c + 1), j0:j1], result[:])

        first = tile("picked1_first", [P, 4, 2 * P], F32, "factor2_7")
        for t in range(4):
            pick(first[:, t, :], windows[4 + t], pos1_sb, factor1[4 + t], 0, 2 * P)
        apply_sign(x2_1[:], x2_abs[:], 1)
        x2_q.append(quantize("x2_q1", x2_1[:], M))
        x1_first = tile("x1_first", [P, 2 * P * 4], BF16)
        weave(x1_first[:], first[:], ACT.Copy)
        x1_q_first = quantize("x1_q_first", x1_first[:], 2 * P)
        for c in range(2):
            finish_product(c, x1_q_first, slice(P * c, P * (c + 1)))

        rest = tile("picked1_rest", [P, 2, 4, P], F32, "x2_abs")
        for c, after in ((2, "x1_q_first_codes"), (3, "x1_q_first_scales")):
            finish_rows(c - 2)
            for t in range(4):
                pick(rest[:, c - 2, t, :], windows[4 + t], pos1_sb, factor1[4 + t], P * c, P * (c + 1))
            x1_c = tile("x1_rest%d" % c, [P, P * 4], BF16, after)
            weave(x1_c[:], rest[:, c - 2], ACT.Copy)
            finish_product(c, quantize("x1_q_rest%d" % c, x1_c[:], P), slice(0, P))
        for c in range(2, 4):
            finish_rows(c)
